import numpy as np
import ml_dtypes


def mxq(x, axis, fmt="e4m3"):
    dtype, down = {"e4m3": (ml_dtypes.float8_e4m3fn, 7), "e5m2": (ml_dtypes.float8_e5m2, 14)}[fmt]
    v = np.moveaxis(np.asarray(x, np.float32).astype(ml_dtypes.bfloat16).astype(np.float64), axis, -1)
    blocks = v.reshape(v.shape[:-1] + (-1, 32))
    amax = np.abs(blocks).max(-1, keepdims=True)
    byte = np.maximum(np.where(amax > 0, np.frexp(amax)[1] - 1 + 127, 0) - down, 1)
    scale = np.exp2(byte - 127.0)
    codes = (blocks / scale).astype(np.float32).astype(dtype).astype(np.float64)
    return np.moveaxis((codes * scale).reshape(v.shape), -1, axis)


WIDE = False


def mx_kscale(k):
    if not WIDE:
        return np.ones(k)
    levels = np.array([30, -30])
    if k % 512:
        return np.exp2(np.random.permutation(np.resize(levels, k // 32))).repeat(32)
    a = np.empty((k // 512, 16))
    for p in range(k // 512):
        a[p, :8] = np.random.permutation(np.resize(levels, 8))
        for g in range(8):
            far = levels[np.abs(levels - a[p, g]) >= 10]
            a[p, g + 8] = far[np.random.randint(len(far))]
    return np.exp2(a.ravel()).repeat(32)


def f64(x):
    return np.asarray(x).astype(np.float64)


def striped(idx):
    return np.tile(np.asarray(idx).reshape(-1, 16).T, (8, 1)).astype(np.uint16)


def unstriped(offs):
    return offs[:16].T.reshape(-1).astype(np.int64)


E2M1 = np.array([0.0, 0.5, 1.0, 1.5, 2.0, 3.0, 4.0, 6.0, -0.0, -0.5, -1.0, -1.5, -2.0, -3.0, -4.0, -6.0])


def pack_weight(w, fmt):
    k, n = w.shape
    w = f64(np.asarray(w, np.float32).astype(ml_dtypes.bfloat16)).reshape(k // 32, 32, n)
    amax = np.abs(w).max(1)
    if fmt in ("e4m3", "e5m2"):
        byte = np.frexp(amax)[1] - 1 + 127 - (7 if fmt == "e4m3" else 14)
    else:
        mant, ex = np.frexp(amax / 6.0)
        byte = np.where(mant > 0.5, ex, ex - 1) + 127
    byte = np.clip(np.where(amax > 0, byte, 1), 1, 254)
    scaled = (w * np.exp2(127.0 - byte)[:, None, :]).reshape(k, n).astype(np.float32)
    by_word = np.ascontiguousarray(scaled.reshape(k // 512, 128, 4, n).transpose(0, 1, 3, 2))
    if fmt in ("e4m3", "e5m2"):
        words = by_word.astype(ml_dtypes.float8_e4m3fn if fmt == "e4m3" else ml_dtypes.float8_e5m2).view(np.uint8)
    else:
        c = by_word.astype(ml_dtypes.float4_e2m1fn).view(np.uint8) & 0xF
        words = (c[..., 0::2] | (c[..., 1::2] << 4)).reshape(k // 512, 128, 2 * n)
    return np.ascontiguousarray(words), np.ascontiguousarray(byte.astype(np.uint8).reshape(k // 512, 16, n))


def unpack_weight(words, scales, fmt):
    g, _, n = scales.shape
    words = np.ascontiguousarray(words).reshape(g, 128, n, -1)
    if fmt in ("e4m3", "e5m2"):
        vals = words.view(ml_dtypes.float8_e4m3fn if fmt == "e4m3" else ml_dtypes.float8_e5m2).astype(np.float64)
    else:
        nib = np.empty((g, 128, n, 4), np.uint8)
        nib[..., 0::2] = words & 0xF
        nib[..., 1::2] = words >> 4
        vals = E2M1[nib]
    vals = vals * np.repeat(np.exp2(scales.astype(np.float64) - 127.0), 8, axis=1)[..., None]
    return vals.transpose(0, 1, 3, 2).reshape(g * 512, n)


def sigmoid(v):
    return 1.0 / (1.0 + np.exp(-v))


K, T, J, S, R, F, Z, G, N, C = 512, 512, 128, 512, 512, 512, 1024, 16, 256, 512


def setup_inputs():
    n = np.random.standard_normal
    idx = np.random.permutation(T)[:J]
    idx2 = np.random.permutation(S)[:J]
    idx3 = np.random.permutation(Z)[:J]
    idx4 = np.random.permutation(C)[:J]
    fk = mx_kscale(K)
    fr = mx_kscale(R)
    ff = mx_kscale(F)
    wp = pack_weight(n((K, R)) * 1 / np.sqrt(K) * fk[:, None] * fr, "e2m1")
    w2p = pack_weight(n((F, R)) * 1 / np.sqrt(F) * ff[:, None] * fr, "e5m2")
    wbp = pack_weight(n((R, N)) * 1 / np.sqrt(R) / fr[:, None], "e5m2")
    return {
        "xa": (n((K, T))).astype(np.float32),
        "xb": (n((K, S))).astype(np.float32),
        "fk": (np.random.uniform(0.5, 2.0, (K, 1)) / fk[:, None]).astype(np.float32),
        "w_words": wp[0],
        "w_scales": wp[1],
        "xo": (n((F, Z))).astype(np.float32),
        "fl": (np.random.uniform(0.5, 2.0, (F, 1)) / ff[:, None]).astype(np.float32),
        "so": (n((F, J))).astype(np.float32),
        "w2_words": w2p[0],
        "w2_scales": w2p[1],
        "wb_words": wbp[0],
        "wb_scales": wbp[1],
        "tz": (n((N, C)) * 0.6).astype(np.float32),
        "rw": (np.random.uniform(0.5, 2.0, (1, J))).astype(np.float32),
        "offs": striped(idx),
        "offs2": striped(idx2),
        "offs3": striped(idx3),
        "offs4": striped(idx4),
    }


def reference(xa, xb, fk, w_words, w_scales, xo, fl, so, w2_words, w2_scales, wb_words, wb_scales, tz, rw, offs, offs2, offs3, offs4):
    idx = unstriped(offs)
    idx2 = unstriped(offs2)
    idx3 = unstriped(offs3)
    idx4 = unstriped(offs4)
    wu = unpack_weight(w_words, w_scales, "e2m1")
    w2u = unpack_weight(w2_words, w2_scales, "e5m2")
    wbu = unpack_weight(wb_words, wb_scales, "e5m2")
    u = f64(xa)[:, idx] * f64(xb)[:, idx2] * f64(fk)
    u2 = f64(xo)[:, idx3] * sigmoid(f64(so)) * f64(fl)
    uq = mxq(u, 0, "e4m3")
    u2q = mxq(u2, 0, "e5m2")
    a = wu.T @ uq + w2u.T @ u2q
    m1 = a.reshape(R, G, J // G).mean(axis=2)
    m2 = np.repeat(m1, J // G, axis=1)
    hid = a - m2
    hidq = mxq(hid, 0, "e5m2")
    p = wbu.T @ hidq
    y = np.maximum(p, f64(tz)[:, idx4]) * f64(rw)
    return y

@@ -1,0 +1,215 @@
+from contextlib import ExitStack
+
+import concourse.mybir as mybir
+from concourse.masks import make_identity
+
+F32 = mybir.dt.float32
+BF16 = mybir.dt.bfloat16
+I32 = mybir.dt.int32
+U32 = mybir.dt.uint32
+U16 = mybir.dt.uint16
+U8 = mybir.dt.uint8
+E4M3 = mybir.dt.float8_e4m3fn_x4
+E5M2 = mybir.dt.float8_e5m2_x4
+E2M1 = mybir.dt.float4_e2m1fn_x4
+ALU = mybir.AluOpType
+ACT = mybir.ActivationFunctionType
+
+P = 128
+PACK = 4
+T, J, S, R, Z, N, C = 512, 128, 512, 512, 1024, 256, 512
+BUNDLE = 8
+HALF = J // 2
+
+FLOPS = 2 * J * (512 * R + 512 * R + R * N)
+
+
+def interleave(copy, dst, src, cols):
+    copy(
+        dst[:, cols, :].rearrange("p (c i) t -> p c t i", i=4),
+        src[:, :, cols].rearrange("p t (c i) -> p c t i", i=4),
+    )
+
+
+def tile_list_sum_entryproducts_gated_levelled_floored_kernel(
+    tc, xa, xb, fk, w_words, w_scales, xo, fl, so, w2_words, w2_scales, wb_words, wb_scales, tz, rw,
+    offs, offs2, offs3, offs4, out,
+):
+    nc = tc.nc
+    with ExitStack() as ctx:
+        sb = ctx.enter_context(tc.tile_pool(name="sb", bufs=1))
+        ps = ctx.enter_context(tc.psum_pool(name="ps", bufs=1))
+
+        list_a = sb.tile([P, J // 16], U16)
+        list_b = sb.tile([P, J // 16], U16)
+        list_o = sb.tile([P, J // 16], U16)
+        list_z = sb.tile([P, J // 16], U16)
+        xa_sb = sb.tile([P, PACK * T], F32)
+        xb_sb = sb.tile([P, PACK * S], F32)
+        xo_sb = [sb.tile([P, Z], F32, name="xo%d" % t) for t in range(PACK)]
+        tz_sb = sb.tile([P, 2 * C], F32)
+        so_sb = sb.tile([P, PACK, J], F32)
+        fk_sb = sb.tile([P, PACK], F32)
+        fl_sb = sb.tile([P, PACK], F32)
+        rw_sb = sb.tile([P, 1], F32)
+        w_raw = sb.tile([P, 2 * R], U8)
+        w2_raw = sb.tile([P, R], U32)
+        wb_sb = sb.tile([P, N], U32, align_bytes=64)
+        sc_all = sb.tile([P, 4 * R + N], U8, align_bytes=64)
+        sc_rows = sc_all[:, 0 : 2 * R + N]
+        sc = sb.tile([P, 2 * R + N], U8, align_bytes=64)
+        sc_raw = sc_all[:, 2 * R + N :]
+
+        nc.scalar.dma_start(so_sb[:], so.rearrange("(p t) j -> p t j", t=PACK))
+        nc.sync.dma_start(xa_sb[:], xa.rearrange("(p t) c -> p (t c)", t=PACK))
+        nc.scalar.dma_start(sc_raw[16:32, 0:R].bitcast(I32), w_scales[0].bitcast(I32))
+        nc.sync.dma_start(list_a[:], offs)
+        nc.scalar.dma_start(sc_raw[16:32, R : 2 * R].bitcast(I32), w2_scales[0].bitcast(I32))
+        nc.sync.dma_start(list_b[:], offs2)
+        nc.gpsimd.dma_start(fk_sb[:], fk.rearrange("(p t) o -> p (t o)", t=PACK))
+        nc.sync.dma_start(xb_sb[:], xb.rearrange("(p t) c -> p (t c)", t=PACK))
+        nc.gpsimd.dma_start(fl_sb[:], fl.rearrange("(p t) o -> p (t o)", t=PACK))
+        nc.sync.dma_start(list_o[:], offs3)
+        nc.gpsimd.dma_start(sc_rows[16:32, 2 * R :].bitcast(I32), wb_scales[0].bitcast(I32))
+        with nc.allow_non_contiguous_dma(reason="one weight a partition"):
+            nc.gpsimd.dma_start(rw_sb[:], rw.rearrange("o j -> j o"))
+        xo_planes = xo.rearrange("(p t) c -> t p c", t=PACK)
+        for t in range(2):
+            nc.sync.dma_start(xo_sb[t][:], xo_planes[t])
+        for rows in (slice(0, 16), slice(32, 64), slice(64, P)):
+            nc.vector.memset(sc_all[rows, 2 * R :].bitcast(I32), 0)
+        nc.vector.tensor_copy(
+            sc_rows[:, 0 : 2 * R].rearrange("p (s t m) -> p s t m", s=2, t=PACK),
+            sc_raw.rearrange("p (s m t) -> p s t m", s=2, t=PACK),
+        )
+        for q in range(4):
+            nc.sync.dma_start(
+                sc[32 * q : 32 * q + 4, :].bitcast(I32), sc_rows[16 + 4 * q : 20 + 4 * q, :].bitcast(I32)
+            )
+
+        for t in range(2, PACK):
+            nc.sync.dma_start(xo_sb[t][:], xo_planes[t])
+        nc.sync.dma_start(w_raw[:].bitcast(I32), w_words[0].bitcast(I32))
+        nc.sync.dma_start(w2_raw[:].bitcast(I32), w2_words[0].rearrange("p n t -> p (n t)").bitcast(I32))
+        nc.sync.dma_start(list_z[:], offs4)
+        nc.sync.dma_start(tz_sb[:].rearrange("p (h c) -> p h c", h=2), tz.rearrange("(h p) c -> p h c", h=2))
+        nc.sync.dma_start(wb_sb[:].bitcast(I32), wb_words[0].rearrange("p n t -> p (n t)").bitcast(I32))
+
+        ident = sb.tile([P, P], F32)
+        make_identity(nc, ident[:])
+        rw_ps = ps.tile([P, J], F32)
+        nc.tensor.transpose(rw_ps[:], rw_sb[:, 0:1].to_broadcast([P, P]), ident[:])
+
+        sig = sb.tile([P, PACK, J], F32)
+        nc.scalar.activation(sig[:], so_sb[:], ACT.Sigmoid)
+        gate = sb.tile([P, PACK, J], F32)
+        nc.vector.tensor_tensor(gate[:], sig[:], fl_sb[:].unsqueeze(2).to_broadcast([P, PACK, J]), ALU.mult)
+
+        ga = sb.tile([P, PACK, J], F32)
+        for t in range(PACK):
+            nc.scalar.activation(ga[:, t, :], xa_sb[:, t * T : (t + 1) * T].indirect(list_a[:]), ACT.Copy)
+        gaf = sb.tile([P, PACK, J], F32)
+        nc.vector.tensor_tensor(gaf[:], ga[:], fk_sb[:].unsqueeze(2).to_broadcast([P, PACK, J]), ALU.mult)
+        gb = sb.tile([P, PACK, J], F32)
+        for t in range(PACK):
+            nc.vector.tensor_copy(gb[:, t, :], xb_sb[:, t * S : (t + 1) * S].indirect(list_b[:]))
+        u = sb.tile([P, PACK, J], F32)
+        nc.vector.tensor_tensor(u[:], gaf[:], gb[:], ALU.mult)
+        u_bf = sb.tile([P, J, PACK], BF16, align_bytes=64)
+        interleave(nc.scalar.copy, u_bf, u, slice(0, J))
+        u_codes = sb.tile([P, J], U32, align_bytes=64)
+        u_sc = sb.tile([P, J], U8, align_bytes=64)
+        nc.vector.quantize_mx(u_codes[:].bitcast(E4M3), u_sc[:], u_bf[:].rearrange("p j t -> p (j t)"))
+
+        halves = [slice(0, HALF), slice(HALF, J)]
+        u2 = sb.tile([P, PACK, J], F32)
+        for t in range(PACK - 1):
+            nc.vector.tensor_tensor(u2[:, t, :], xo_sb[t][:].indirect(list_o[:]), gate[:, t, :], ALU.mult)
+        for i, cols in enumerate(halves):
+            nc.vector.tensor_tensor(
+                u2[:, PACK - 1, cols], xo_sb[PACK - 1][:].indirect(list_o[:, 4 * i : 4 * i + 4]),
+                gate[:, PACK - 1, cols], ALU.mult,
+            )
+        u2_bf = sb.tile([P, J, PACK], BF16, align_bytes=64)
+        for cols in halves:
+            interleave(nc.vector.tensor_copy, u2_bf, u2, cols)
+        u2_codes = sb.tile([P, J], U32, align_bytes=64)
+        u2_sc = sb.tile([P, J], U8, align_bytes=64)
+        for cols in halves:
+            nc.vector.quantize_mx(
+                u2_codes[:, cols].bitcast(E5M2), u2_sc[:, cols], u2_bf[:, cols, :].rearrange("p j t -> p (j t)")
+            )
+
+        w_sb = sb.tile([P, 2 * R], U8, align_bytes=64)
+        nc.scalar.copy(
+            w_sb[:].bitcast(U16).rearrange("p (t m) -> p t m", t=PACK),
+            w_raw[:].bitcast(U16).rearrange("p (m t) -> p t m", t=PACK),
+        )
+        w2_sb = sb.tile([P, R], U32, align_bytes=64)
+        nc.scalar.copy(
+            w2_sb[:].rearrange("p (t m) -> p t m", t=PACK),
+            w2_raw[:].rearrange("p (m t) -> p t m", t=PACK),
+        )
+
+        acc = ps.tile([P, PACK * J], F32)
+        for t in range(PACK):
+            nc.tensor.matmul_mx(
+                out=acc[:, t * J : (t + 1) * J],
+                lhsT=w_sb[:, 2 * P * t : 2 * P * (t + 1)].bitcast(E2M1), lhsT_scale=sc[:, P * t : P * (t + 1)],
+                rhs=u_codes[:].bitcast(E4M3), rhs_scale=u_sc[:],
+                start=(t == 0), stop=False,
+            )
+        for t in range(PACK):
+            nc.tensor.matmul_mx(
+                out=acc[:, t * J : (t + 1) * J],
+                lhsT=w2_sb[:, P * t : P * (t + 1)].bitcast(E5M2), lhsT_scale=sc[:, R + P * t : R + P * (t + 1)],
+                rhs=u2_codes[:].bitcast(E5M2), rhs_scale=u2_sc[:],
+                start=False, stop=(t == PACK - 1),
+            )
+
+        gz = sb.tile([P, 2, J], F32)
+        for h in range(2):
+            nc.scalar.activation(gz[:, h, :], tz_sb[:, h * C : (h + 1) * C].indirect(list_z[:]), ACT.Copy)
+
+        groups = HALF // BUNDLE
+        a_view = acc[:].rearrange("p (t j) -> p t j", t=PACK)
+        sums = [sb.tile([P, groups, PACK], F32, name="sums%d" % i) for i in range(2)]
+        means = [sb.tile([P, groups, PACK], F32, name="means%d" % i) for i in range(2)]
+        for i, cols in enumerate(halves):
+            nc.vector.tensor_reduce(
+                sums[i][:], a_view[:, :, cols].rearrange("p t (g e) -> p g t e", e=BUNDLE),
+                mybir.AxisListType.X, ALU.add,
+            )
+            nc.scalar.activation(means[i][:], sums[i][:], ACT.Copy, scale=1.0 / BUNDLE)
+        hid_bf = sb.tile([P, J, PACK], BF16, align_bytes=64)
+        for i, cols in enumerate(halves):
+            nc.vector.tensor_tensor(
+                hid_bf[:, cols, :].rearrange("p (g e) t -> p g e t", e=BUNDLE),
+                a_view[:, :, cols].rearrange("p t (g e) -> p g e t", e=BUNDLE),
+                means[i][:].unsqueeze(2).to_broadcast([P, groups, BUNDLE, PACK]),
+                ALU.subtract,
+            )
+        hid_codes = sb.tile([P, J], U32, align_bytes=64)
+        hid_sc = sb.tile([P, J], U8, align_bytes=64)
+        for cols in halves:
+            nc.vector.quantize_mx(
+                hid_codes[:, cols].bitcast(E5M2), hid_sc[:, cols], hid_bf[:, cols, :].rearrange("p j t -> p (j t)")
+            )
+
+        prod = [ps.tile([P, J], F32, name="prod%d" % h) for h in range(2)]
+        top = sb.tile([P, 2, J], F32)
+        y = [sb.tile([P, J], F32, name="y%d" % h) for h in range(2)]
+        for h in range(2):
+            nc.tensor.matmul_mx(
+                out=prod[h][:],
+                lhsT=wb_sb[:, P * h : P * (h + 1)].bitcast(E5M2),
+                lhsT_scale=sc[:, 2 * R + P * h : 2 * R + P * (h + 1)],
+                rhs=hid_codes[:].bitcast(E5M2), rhs_scale=hid_sc[:],
+                start=True, stop=True,
+            )
+        for h in range(2):
+            nc.vector.tensor_tensor(top[:, h, :], prod[h][:], gz[:, h, :], ALU.max)
+        for h in range(2):
+            nc.vector.tensor_tensor(y[h][:], top[:, h, :], rw_ps[:], ALU.mult)
+        nc.scalar.dma_start(out[0:P, :], y[0][:])
+        nc.sync.dma_start(out[P : 2 * P, :], y[1][:])

@@ -26,8 +26,8 @@ FLOPS = 2 * J * (512 * R + 512 * R + R * N)
 
 def interleave(copy, dst, src, cols):
     copy(
-        dst[:, cols, :].rearrange("p (c i) t -> p c t i", i=4),
-        src[:, :, cols].rearrange("p t (c i) -> p c t i", i=4),
+        dst[:, cols, :].rearrange("p (c i g) t -> p c g t i", c=2, i=4),
+        src[:, :, cols].rearrange("p t (g c i) -> p c g t i", c=2, i=4),
     )
 
 
@@ -69,8 +69,8 @@ def tile_list_sum_entryproducts_gated_levelled_floored_kernel(
         nc.gpsimd.dma_start(fk_sb[:], fk.rearrange("(p t) o -> p (t o)", t=PACK))
         nc.sync.dma_start(xb_sb[:], xb.rearrange("(p t) c -> p (t c)", t=PACK))
         nc.gpsimd.dma_start(fl_sb[:], fl.rearrange("(p t) o -> p (t o)", t=PACK))
+        nc.scalar.dma_start(sc_rows[16:32, 2 * R :].bitcast(I32), wb_scales[0].bitcast(I32))
         nc.sync.dma_start(list_o[:], offs3)
-        nc.gpsimd.dma_start(sc_rows[16:32, 2 * R :].bitcast(I32), wb_scales[0].bitcast(I32))
         with nc.allow_non_contiguous_dma(reason="one weight a partition"):
             nc.gpsimd.dma_start(rw_sb[:], rw.rearrange("o j -> j o"))
         xo_planes = xo.rearrange("(p t) c -> t p c", t=PACK)
@@ -116,12 +116,13 @@ def tile_list_sum_entryproducts_gated_levelled_floored_kernel(
         u = sb.tile([P, PACK, J], F32)
         nc.vector.tensor_tensor(u[:], gaf[:], gb[:], ALU.mult)
         u_bf = sb.tile([P, J, PACK], BF16, align_bytes=64)
-        interleave(nc.scalar.copy, u_bf, u, slice(0, J))
+        halves = [slice(0, HALF), slice(HALF, J)]
+        for cols in halves:
+            interleave(nc.scalar.copy, u_bf, u, cols)
         u_codes = sb.tile([P, J], U32, align_bytes=64)
         u_sc = sb.tile([P, J], U8, align_bytes=64)
         nc.vector.quantize_mx(u_codes[:].bitcast(E4M3), u_sc[:], u_bf[:].rearrange("p j t -> p (j t)"))
 
-        halves = [slice(0, HALF), slice(HALF, J)]
         u2 = sb.tile([P, PACK, J], F32)
         for t in range(PACK - 1):
             nc.vector.tensor_tensor(u2[:, t, :], xo_sb[t][:].indirect(list_o[:]), gate[:, t, :], ALU.mult)
@@ -142,13 +143,13 @@ def tile_list_sum_entryproducts_gated_levelled_floored_kernel(
 
         w_sb = sb.tile([P, 2 * R], U8, align_bytes=64)
         nc.scalar.copy(
-            w_sb[:].bitcast(U16).rearrange("p (t m) -> p t m", t=PACK),
-            w_raw[:].bitcast(U16).rearrange("p (m t) -> p t m", t=PACK),
+            w_sb[:].bitcast(U16).rearrange("p (t m) -> p m t", t=PACK),
+            w_raw[:].bitcast(U16).rearrange("p (m t) -> p m t", t=PACK),
         )
         w2_sb = sb.tile([P, R], U32, align_bytes=64)
         nc.scalar.copy(
-            w2_sb[:].rearrange("p (t m) -> p t m", t=PACK),
-            w2_raw[:].rearrange("p (m t) -> p t m", t=PACK),
+            w2_sb[:].rearrange("p (t m) -> p m t", t=PACK),
+            w2_raw[:].rearrange("p (m t) -> p m t", t=PACK),
         )
 
         acc = ps.tile([P, PACK * J], F32)
@@ -174,20 +175,19 @@ def tile_list_sum_entryproducts_gated_levelled_floored_kernel(
         groups = HALF // BUNDLE
         a_view = acc[:].rearrange("p (t j) -> p t j", t=PACK)
         sums = [sb.tile([P, groups, PACK], F32, name="sums%d" % i) for i in range(2)]
-        means = [sb.tile([P, groups, PACK], F32, name="means%d" % i) for i in range(2)]
         for i, cols in enumerate(halves):
             nc.vector.tensor_reduce(
-                sums[i][:], a_view[:, :, cols].rearrange("p t (g e) -> p g t e", e=BUNDLE),
+                sums[i][:], a_view[:, :, cols].rearrange("p t (e g) -> p g t e", e=BUNDLE),
                 mybir.AxisListType.X, ALU.add,
             )
-            nc.scalar.activation(means[i][:], sums[i][:], ACT.Copy, scale=1.0 / BUNDLE)
         hid_bf = sb.tile([P, J, PACK], BF16, align_bytes=64)
         for i, cols in enumerate(halves):
-            nc.vector.tensor_tensor(
-                hid_bf[:, cols, :].rearrange("p (g e) t -> p g e t", e=BUNDLE),
-                a_view[:, :, cols].rearrange("p t (g e) -> p g e t", e=BUNDLE),
-                means[i][:].unsqueeze(2).to_broadcast([P, groups, BUNDLE, PACK]),
-                ALU.subtract,
+            nc.vector.scalar_tensor_tensor(
+                hid_bf[:, cols, :].rearrange("p (e g) t -> p e g t", e=BUNDLE),
+                sums[i][:].unsqueeze(1).to_broadcast([P, BUNDLE, groups, PACK]),
+                -1.0 / BUNDLE,
+                a_view[:, :, cols].rearrange("p t (e g) -> p e g t", e=BUNDLE),
+                ALU.mult, ALU.add,
             )
         hid_codes = sb.tile([P, J], U32, align_bytes=64)
         hid_sc = sb.tile([P, J], U8, align_bytes=64)
@@ -208,7 +208,12 @@ def tile_list_sum_entryproducts_gated_levelled_floored_kernel(
                 start=True, stop=True,
             )
         for h in range(2):
-            nc.vector.tensor_tensor(top[:, h, :], prod[h][:], gz[:, h, :], ALU.max)
+            nc.vector.tensor_tensor(
+                top[:, h, :].rearrange("p (i g e) -> p i g e", i=2, e=BUNDLE),
+                prod[h][:].rearrange("p (i e g) -> p i g e", i=2, e=BUNDLE),
+                gz[:, h, :].rearrange("p (i g e) -> p i g e", i=2, e=BUNDLE),
+                ALU.max,
+            )
         for h in range(2):
             nc.vector.tensor_tensor(y[h][:], top[:, h, :], rw_ps[:], ALU.mult)
         nc.scalar.dma_start(out[0:P, :], y[0][:])

from contextlib import ExitStack

import concourse.mybir as mybir
from concourse.masks import make_identity

F32 = mybir.dt.float32
BF16 = mybir.dt.bfloat16
I32 = mybir.dt.int32
U32 = mybir.dt.uint32
U16 = mybir.dt.uint16
U8 = mybir.dt.uint8
E4M3 = mybir.dt.float8_e4m3fn_x4
E5M2 = mybir.dt.float8_e5m2_x4
E2M1 = mybir.dt.float4_e2m1fn_x4
ALU = mybir.AluOpType
ACT = mybir.ActivationFunctionType

P = 128
PACK = 4
T, J, S, R, Z, N, C = 512, 128, 512, 512, 1024, 256, 512
BUNDLE = 8
HALF = J // 2

FLOPS = 2 * J * (512 * R + 512 * R + R * N)


def interleave(copy, dst, src, cols):
    copy(
        dst[:, cols, :].rearrange("p (c i g) t -> p c g t i", c=2, i=4),
        src[:, :, cols].rearrange("p t (g c i) -> p c g t i", c=2, i=4),
    )


def tile_list_sum_entryproducts_gated_levelled_floored_kernel(
    tc, xa, xb, fk, w_words, w_scales, xo, fl, so, w2_words, w2_scales, wb_words, wb_scales, tz, rw,
    offs, offs2, offs3, offs4, out,
):
    nc = tc.nc
    with ExitStack() as ctx:
        sb = ctx.enter_context(tc.tile_pool(name="sb", bufs=1))
        ps = ctx.enter_context(tc.psum_pool(name="ps", bufs=1))

        list_a = sb.tile([P, J // 16], U16)
        list_b = sb.tile([P, J // 16], U16)
        list_o = sb.tile([P, J // 16], U16)
        list_z = sb.tile([P, J // 16], U16)
        xa_sb = sb.tile([P, PACK * T], F32)
        xb_sb = sb.tile([P, PACK * S], F32)
        xo_sb = [sb.tile([P, Z], F32, name="xo%d" % t) for t in range(PACK)]
        tz_sb = sb.tile([P, 2 * C], F32)
        so_sb = sb.tile([P, PACK, J], F32)
        fk_sb = sb.tile([P, PACK], F32)
        fl_sb = sb.tile([P, PACK], F32)
        rw_sb = sb.tile([P, 1], F32)
        w_raw = sb.tile([P, 2 * R], U8)
        w2_raw = sb.tile([P, R], U32)
        wb_sb = sb.tile([P, N], U32, align_bytes=64)
        sc_all = sb.tile([P, 4 * R + N], U8, align_bytes=64)
        sc_rows = sc_all[:, 0 : 2 * R + N]
        sc = sb.tile([P, 2 * R + N], U8, align_bytes=64)
        sc_raw = sc_all[:, 2 * R + N :]

        nc.scalar.dma_start(so_sb[:], so.rearrange("(p t) j -> p t j", t=PACK))
        nc.sync.dma_start(xa_sb[:], xa.rearrange("(p t) c -> p (t c)", t=PACK))
        nc.scalar.dma_start(sc_raw[16:32, 0:R].bitcast(I32), w_scales[0].bitcast(I32))
        nc.sync.dma_start(list_a[:], offs)
        nc.scalar.dma_start(sc_raw[16:32, R : 2 * R].bitcast(I32), w2_scales[0].bitcast(I32))
        nc.sync.dma_start(list_b[:], offs2)
        nc.gpsimd.dma_start(fk_sb[:], fk.rearrange("(p t) o -> p (t o)", t=PACK))
        nc.sync.dma_start(xb_sb[:], xb.rearrange("(p t) c -> p (t c)", t=PACK))
        nc.gpsimd.dma_start(fl_sb[:], fl.rearrange("(p t) o -> p (t o)", t=PACK))
        nc.scalar.dma_start(sc_rows[16:32, 2 * R :].bitcast(I32), wb_scales[0].bitcast(I32))
        nc.sync.dma_start(list_o[:], offs3)
        with nc.allow_non_contiguous_dma(reason="one weight a partition"):
            nc.gpsimd.dma_start(rw_sb[:], rw.rearrange("o j -> j o"))
        xo_planes = xo.rearrange("(p t) c -> t p c", t=PACK)
        for t in range(2):
            nc.sync.dma_start(xo_sb[t][:], xo_planes[t])
        for rows in (slice(0, 16), slice(32, 64), slice(64, P)):
            nc.vector.memset(sc_all[rows, 2 * R :].bitcast(I32), 0)
        nc.vector.tensor_copy(
            sc_rows[:, 0 : 2 * R].rearrange("p (s t m) -> p s t m", s=2, t=PACK),
            sc_raw.rearrange("p (s m t) -> p s t m", s=2, t=PACK),
        )
        for q in range(4):
            nc.sync.dma_start(
                sc[32 * q : 32 * q + 4, :].bitcast(I32), sc_rows[16 + 4 * q : 20 + 4 * q, :].bitcast(I32)
            )

        for t in range(2, PACK):
            nc.sync.dma_start(xo_sb[t][:], xo_planes[t])
        nc.sync.dma_start(w_raw[:].bitcast(I32), w_words[0].bitcast(I32))
        nc.sync.dma_start(w2_raw[:].bitcast(I32), w2_words[0].rearrange("p n t -> p (n t)").bitcast(I32))
        nc.sync.dma_start(list_z[:], offs4)
        nc.sync.dma_start(tz_sb[:].rearrange("p (h c) -> p h c", h=2), tz.rearrange("(h p) c -> p h c", h=2))
        nc.sync.dma_start(wb_sb[:].bitcast(I32), wb_words[0].rearrange("p n t -> p (n t)").bitcast(I32))

        ident = sb.tile([P, P], F32)
        make_identity(nc, ident[:])
        rw_ps = ps.tile([P, J], F32)
        nc.tensor.transpose(rw_ps[:], rw_sb[:, 0:1].to_broadcast([P, P]), ident[:])

        sig = sb.tile([P, PACK, J], F32)
        nc.scalar.activation(sig[:], so_sb[:], ACT.Sigmoid)
        gate = sb.tile([P, PACK, J], F32)
        nc.vector.tensor_tensor(gate[:], sig[:], fl_sb[:].unsqueeze(2).to_broadcast([P, PACK, J]), ALU.mult)

        ga = sb.tile([P, PACK, J], F32)
        for t in range(PACK):
            nc.scalar.activation(ga[:, t, :], xa_sb[:, t * T : (t + 1) * T].indirect(list_a[:]), ACT.Copy)
        gaf = sb.tile([P, PACK, J], F32)
        nc.vector.tensor_tensor(gaf[:], ga[:], fk_sb[:].unsqueeze(2).to_broadcast([P, PACK, J]), ALU.mult)
        gb = sb.tile([P, PACK, J], F32)
        for t in range(PACK):
            nc.vector.tensor_copy(gb[:, t, :], xb_sb[:, t * S : (t + 1) * S].indirect(list_b[:]))
        u = sb.tile([P, PACK, J], F32)
        nc.vector.tensor_tensor(u[:], gaf[:], gb[:], ALU.mult)
        u_bf = sb.tile([P, J, PACK], BF16, align_bytes=64)
        halves = [slice(0, HALF), slice(HALF, J)]
        for cols in halves:
            interleave(nc.scalar.copy, u_bf, u, cols)
        u_codes = sb.tile([P, J], U32, align_bytes=64)
        u_sc = sb.tile([P, J], U8, align_bytes=64)
        nc.vector.quantize_mx(u_codes[:].bitcast(E4M3), u_sc[:], u_bf[:].rearrange("p j t -> p (j t)"))

        u2 = sb.tile([P, PACK, J], F32)
        for t in range(PACK - 1):
            nc.vector.tensor_tensor(u2[:, t, :], xo_sb[t][:].indirect(list_o[:]), gate[:, t, :], ALU.mult)
        for i, cols in enumerate(halves):
            nc.vector.tensor_tensor(
                u2[:, PACK - 1, cols], xo_sb[PACK - 1][:].indirect(list_o[:, 4 * i : 4 * i + 4]),
                gate[:, PACK - 1, cols], ALU.mult,
            )
        u2_bf = sb.tile([P, J, PACK], BF16, align_bytes=64)
        for cols in halves:
            interleave(nc.vector.tensor_copy, u2_bf, u2, cols)
        u2_codes = sb.tile([P, J], U32, align_bytes=64)
        u2_sc = sb.tile([P, J], U8, align_bytes=64)
        for cols in halves:
            nc.vector.quantize_mx(
                u2_codes[:, cols].bitcast(E5M2), u2_sc[:, cols], u2_bf[:, cols, :].rearrange("p j t -> p (j t)")
            )

        w_sb = sb.tile([P, 2 * R], U8, align_bytes=64)
        nc.scalar.copy(
            w_sb[:].bitcast(U16).rearrange("p (t m) -> p m t", t=PACK),
            w_raw[:].bitcast(U16).rearrange("p (m t) -> p m t", t=PACK),
        )
        w2_sb = sb.tile([P, R], U32, align_bytes=64)
        nc.scalar.copy(
            w2_sb[:].rearrange("p (t m) -> p m t", t=PACK),
            w2_raw[:].rearrange("p (m t) -> p m t", t=PACK),
        )

        acc = ps.tile([P, PACK * J], F32)
        for t in range(PACK):
            nc.tensor.matmul_mx(
                out=acc[:, t * J : (t + 1) * J],
                lhsT=w_sb[:, 2 * P * t : 2 * P * (t + 1)].bitcast(E2M1), lhsT_scale=sc[:, P * t : P * (t + 1)],
                rhs=u_codes[:].bitcast(E4M3), rhs_scale=u_sc[:],
                start=(t == 0), stop=False,
            )
        for t in range(PACK):
            nc.tensor.matmul_mx(
                out=acc[:, t * J : (t + 1) * J],
                lhsT=w2_sb[:, P * t : P * (t + 1)].bitcast(E5M2), lhsT_scale=sc[:, R + P * t : R + P * (t + 1)],
                rhs=u2_codes[:].bitcast(E5M2), rhs_scale=u2_sc[:],
                start=False, stop=(t == PACK - 1),
            )

        gz = sb.tile([P, 2, J], F32)
        for h in range(2):
            nc.scalar.activation(gz[:, h, :], tz_sb[:, h * C : (h + 1) * C].indirect(list_z[:]), ACT.Copy)

        groups = HALF // BUNDLE
        a_view = acc[:].rearrange("p (t j) -> p t j", t=PACK)
        sums = [sb.tile([P, groups, PACK], F32, name="sums%d" % i) for i in range(2)]
        for i, cols in enumerate(halves):
            nc.vector.tensor_reduce(
                sums[i][:], a_view[:, :, cols].rearrange("p t (e g) -> p g t e", e=BUNDLE),
                mybir.AxisListType.X, ALU.add,
            )
        hid_bf = sb.tile([P, J, PACK], BF16, align_bytes=64)
        for i, cols in enumerate(halves):
            nc.vector.scalar_tensor_tensor(
                hid_bf[:, cols, :].rearrange("p (e g) t -> p e g t", e=BUNDLE),
                sums[i][:].unsqueeze(1).to_broadcast([P, BUNDLE, groups, PACK]),
                -1.0 / BUNDLE,
                a_view[:, :, cols].rearrange("p t (e g) -> p e g t", e=BUNDLE),
                ALU.mult, ALU.add,
            )
        hid_codes = sb.tile([P, J], U32, align_bytes=64)
        hid_sc = sb.tile([P, J], U8, align_bytes=64)
        for cols in halves:
            nc.vector.quantize_mx(
                hid_codes[:, cols].bitcast(E5M2), hid_sc[:, cols], hid_bf[:, cols, :].rearrange("p j t -> p (j t)")
            )

        prod = [ps.tile([P, J], F32, name="prod%d" % h) for h in range(2)]
        top = sb.tile([P, 2, J], F32)
        y = [sb.tile([P, J], F32, name="y%d" % h) for h in range(2)]
        for h in range(2):
            nc.tensor.matmul_mx(
                out=prod[h][:],
                lhsT=wb_sb[:, P * h : P * (h + 1)].bitcast(E5M2),
                lhsT_scale=sc[:, 2 * R + P * h : 2 * R + P * (h + 1)],
                rhs=hid_codes[:].bitcast(E5M2), rhs_scale=hid_sc[:],
                start=True, stop=True,
            )
        for h in range(2):
            nc.vector.tensor_tensor(
                top[:, h, :].rearrange("p (i g e) -> p i g e", i=2, e=BUNDLE),
                prod[h][:].rearrange("p (i e g) -> p i g e", i=2, e=BUNDLE),
                gz[:, h, :].rearrange("p (i g e) -> p i g e", i=2, e=BUNDLE),
                ALU.max,
            )
        for h in range(2):
            nc.vector.tensor_tensor(y[h][:], top[:, h, :], rw_ps[:], ALU.mult)
        nc.scalar.dma_start(out[0:P, :], y[0][:])
        nc.sync.dma_start(out[P : 2 * P, :], y[1][:])
